import numpy as np
import ml_dtypes


def mxq(x, axis, fmt="e4m3"):
    dtype, down = {"e4m3": (ml_dtypes.float8_e4m3fn, 7), "e5m2": (ml_dtypes.float8_e5m2, 14)}[fmt]
    v = np.moveaxis(np.asarray(x, np.float32).astype(ml_dtypes.bfloat16).astype(np.float64), axis, -1)
    blocks = v.reshape(v.shape[:-1] + (-1, 32))
    amax = np.abs(blocks).max(-1, keepdims=True)
    byte = np.maximum(np.where(amax > 0, np.frexp(amax)[1] - 1 + 127, 0) - down, 1)
    scale = np.exp2(byte - 127.0)
    codes = (blocks / scale).astype(np.float32).astype(dtype).astype(np.float64)
    return np.moveaxis((codes * scale).reshape(v.shape), -1, axis)


WIDE = False


def mx_kscale(k):
    if not WIDE:
        return np.ones(k)
    levels = np.array([10, -10, 5, -5, 0])
    if k % 512:
        return np.exp2(np.random.permutation(np.resize(levels, k // 32))).repeat(32)
    a = np.empty((k // 512, 16))
    for p in range(k // 512):
        a[p, :8] = np.random.permutation(np.resize(levels, 8))
        for g in range(8):
            far = levels[np.abs(levels - a[p, g]) >= 10]
            a[p, g + 8] = far[np.random.randint(len(far))]
    return np.exp2(a.ravel()).repeat(32)


def f64(x):
    return np.asarray(x).astype(np.float64)


def striped(idx):
    return np.tile(idx.reshape(-1, 16).T, (8, 1)).astype(np.uint16)


def unstriped(offs):
    return offs[:16].T.reshape(-1).astype(np.int64)


def pack_weight(w):
    k, n = w.shape
    w = f64(np.asarray(w, np.float32).astype(ml_dtypes.bfloat16)).reshape(k // 32, 32, n)
    amax = np.abs(w).max(1)
    byte = np.clip(np.where(amax > 0, np.frexp(amax)[1] - 1 + 127 - 7, 1), 1, 254)
    scaled = (w * np.exp2(127.0 - byte)[:, None, :]).reshape(k, n).astype(np.float32)
    words = np.ascontiguousarray(scaled.reshape(k // 512, 128, 4, n).transpose(0, 1, 3, 2)).astype(ml_dtypes.float8_e4m3fn).view(np.uint8)
    return words, np.ascontiguousarray(byte.astype(np.uint8).reshape(k // 512, 16, n))


def unpack_weight(words, scales):
    g, p, n, _ = words.shape
    vals = np.ascontiguousarray(words).view(ml_dtypes.float8_e4m3fn).astype(np.float64) * np.repeat(np.exp2(scales.astype(np.float64) - 127.0), 8, axis=1)[..., None]
    return vals.transpose(0, 1, 3, 2).reshape(g * 512, n)


def planes(y):
    n, m = y.shape
    v = y.astype(np.float32).astype(ml_dtypes.bfloat16).astype(np.float64).reshape(n // 32, 32, m)
    top = np.abs(v).max(1)
    byte = np.clip(np.where(top > 0, np.frexp(top)[1] - 1 + 127 - 7, 1), 1, 254)
    codes = (v * np.exp2(127.0 - byte)[:, None, :]).reshape(n, m).astype(np.float32).astype(ml_dtypes.float8_e4m3fn).view(np.uint8)
    words = codes.reshape(n // 512, 128, 4, m).transpose(0, 1, 3, 2)
    return np.ascontiguousarray(words), np.ascontiguousarray(byte.astype(np.uint8).reshape(n // 512, 16, m))


K, T, S, V, H, N = 512, 2048, 512, 256, 512, 512


def setup_inputs():
    n = np.random.standard_normal
    s = mx_kscale(K)[:, None]
    u = mx_kscale(H)
    near = np.random.permutation(S)
    packed_xT = pack_weight(n((K, T)) * s)
    packed_w1 = pack_weight(n((K, N)) / np.sqrt(K) / s)
    packed_w2 = pack_weight(n((K, N)) / np.sqrt(K) / s)
    packed_w4 = pack_weight(n((H, N)) / np.sqrt(H) / u[:, None])
    return {
        "x_words": packed_xT[0],
        "x_scales": packed_xT[1],
        "w1_words": packed_w1[0],
        "w1_scales": packed_w1[1],
        "w2_words": packed_w2[0],
        "w2_scales": packed_w2[1],
        "w3": (n((K, H)) / np.sqrt(K) / s * u).astype(np.float32),
        "w4_words": packed_w4[0],
        "w4_scales": packed_w4[1],
        "offs": striped(np.random.permutation(T)[:S]),
        "cen": striped(np.random.permutation(S)[:V]),
        "pos1": striped(near[:V]),
        "pos2": striped(near[V:]),
        "pos3": striped(np.random.permutation(S)[:V]),
    }


def reference(x_words, x_scales, w1_words, w1_scales, w2_words, w2_scales, w3, w4_words, w4_scales, offs, cen, pos1, pos2, pos3):
    xq = unpack_weight(x_words, x_scales)[:, unstriped(offs)]
    h = mxq(f64(w3), 0, "e4m3").T @ xq
    y = unpack_weight(w1_words, w1_scales).T @ xq
    yc = y[:, unstriped(cen)]
    e = unpack_weight(w2_words, w2_scales).T @ xq
    a0 = np.exp(-1.0 * (np.abs(yc - e[:, unstriped(pos1)])))
    a1 = np.exp(-1.0 * (np.abs(yc - e[:, unstriped(pos2)])))
    a2 = np.exp(-1.0 * (np.abs(yc - e[:, unstriped(pos3)])))
    num = h[:, unstriped(pos1)] * a0 + h[:, unstriped(pos2)] * a1 + h[:, unstriped(pos3)] * a2
    den = a0 + a1 + a2
    z = num / den
    out_0 = unpack_weight(w4_words, w4_scales).T @ mxq(z, 0, "e4m3")
    return (out_0,) + planes(out_0)

@@ -1,0 +1,250 @@
+from contextlib import ExitStack
+
+import concourse.mybir as mybir
+from concourse.masks import make_identity
+
+K, T, S, V, H, N = 512, 2048, 512, 256, 512, 512
+FLOPS = 2 * K * S * (N + N + H) + 2 * H * N * V
+
+F32 = mybir.dt.float32
+BF16 = mybir.dt.bfloat16
+I32 = mybir.dt.int32
+U32 = mybir.dt.uint32
+U16 = mybir.dt.uint16
+U8 = mybir.dt.uint8
+FP8X4 = mybir.dt.float8_e4m3fn_x4
+ACT = mybir.ActivationFunctionType
+ALU = mybir.AluOpType
+
+P = 128
+PACK = 4
+BLOCKS = H // P
+HALVES = V // P
+NEIGHBOURS = 3
+QUADRANTS = 4
+
+
+def tile_picked_zpt_lap_po_kernel(
+    tc, x_words, x_scales, w1_words, w1_scales, w2_words, w2_scales, w3, w4_words, w4_scales,
+    offs, cen, pos1, pos2, pos3, out_0, out_1, out_2,
+):
+    nc = tc.nc
+
+    with ExitStack() as ctx:
+        keep = ctx.enter_context(tc.tile_pool(name="keep", bufs=1))
+        psum = ctx.enter_context(tc.psum_pool(name="psum", bufs=1))
+
+        def sbuf(name, shape, dtype, tag=None):
+            return keep.tile(shape, dtype, name=name, tag=tag or name, align_bytes=64)
+
+        def load_words(tile, words):
+            nc.sync.dma_start(out=tile[:].bitcast(I32), in_=words[0].rearrange("p n t -> p (n t)").bitcast(I32))
+
+        def load_scales(queue, plane, scales):
+            for q in range(QUADRANTS):
+                queue.dma_start(out=plane[32 * q : 32 * q + 4, :].bitcast(I32), in_=scales[0][4 * q : 4 * q + 4, :].bitcast(I32))
+
+        def load_list(name, dram, entries):
+            tile = keep.tile([P, entries // 16], U16, name=name)
+            nc.sync.dma_start(tile[:], dram)
+            return tile
+
+        banks = [psum.tile([P, 512], F32, name="bank%d" % b) for b in range(8)]
+
+        x_plane = sbuf("x_plane", [P, T], U8, tag="x_plane_bytes")
+        w_planes = sbuf("w_planes", [P, 3 * N], U8)
+        nc.vector.memset(x_plane[:].bitcast(I32), 0)
+        nc.gpsimd.memset(w_planes[:].bitcast(I32), 0)
+        w1_plane, w2_plane, w4_plane = (w_planes[:, j * N : (j + 1) * N] for j in range(3))
+
+        offs_t = load_list("offs_t", offs, S)
+        cen_t = load_list("cen_t", cen, V)
+        pos_t = [load_list("pos%d_t" % d, pos, V) for d, pos in enumerate((pos1, pos2, pos3))]
+        x_codes = sbuf("x_codes", [P, T], U32, tag="x_codes_bytes")
+        load_words(x_codes, x_words)
+        w1_codes = sbuf("w1_codes", [P, N], U32)
+        load_words(w1_codes, w1_words)
+        w2_codes = sbuf("w2_codes", [P, N], U32)
+        load_words(w2_codes, w2_words)
+        load_scales(nc.sync, x_plane[:], x_scales)
+        load_scales(nc.sync, w1_plane, w1_scales)
+        load_scales(nc.sync, w2_plane, w2_scales)
+        load_scales(nc.gpsimd, w4_plane, w4_scales)
+
+        ident = sbuf("ident", [P, P], F32)
+        make_identity(nc, ident[:])
+
+        xq_codes = sbuf("xq_codes", [P, S], U32)
+        nc.vector.tensor_copy(out=xq_codes[:], in_=x_codes[:].indirect(offs_t[:]))
+        xq_plane = sbuf("xq_plane", [P, S], U8)
+        nc.vector.tensor_copy(out=xq_plane[:], in_=x_plane[:].indirect(offs_t[:]))
+
+        w3_raw = sbuf("w3_raw", [P, PACK, H], F32, tag="x_codes_bytes")
+        nc.sync.dma_start(out=w3_raw[:], in_=w3.rearrange("(p j) c -> p j c", j=PACK))
+        w4_codes = sbuf("w4_codes", [P, N], U32, tag="x_plane_bytes")
+        load_words(w4_codes, w4_words)
+
+        def product(bank, codes, plane, b):
+            cols = slice(P * b, P * (b + 1))
+            nc.tensor.matmul_mx(
+                out=bank[:], lhsT=codes[:, cols].bitcast(FP8X4), lhsT_scale=plane[:, cols],
+                rhs=xq_codes[:].bitcast(FP8X4), rhs_scale=xq_plane[:], start=True, stop=True,
+            )
+
+        y = [sbuf("y%d" % b, [P, S], F32) for b in range(BLOCKS)]
+        e = [sbuf("e%d" % b, [P, S], F32) for b in range(BLOCKS)]
+        h = [sbuf("h%d" % b, [P, S], F32) for b in range(BLOCKS)]
+        yc = [sbuf("yc%d" % b, [P, V], F32) for b in range(BLOCKS)]
+        diff = [sbuf("diff%d" % b, [P, NEIGHBOURS, V], F32) for b in range(BLOCKS)]
+        dist = [sbuf("dist%d" % b, [P, NEIGHBOURS, V], F32) for b in range(BLOCKS)]
+        near2 = [sbuf("near2_%d" % b, [P, V], F32) for b in range(BLOCKS)]
+        near3 = [sbuf("near3_%d" % b, [P, V], F32) for b in range(BLOCKS)]
+        excess = [sbuf("excess%d" % b, [P, NEIGHBOURS, V], F32) for b in range(BLOCKS)]
+        weight = [sbuf("weight%d" % b, [P, NEIGHBOURS, V], F32) for b in range(BLOCKS)]
+        term = [sbuf("term%d" % b, [P, NEIGHBOURS, V], F32) for b in range(BLOCKS)]
+        num_banks = banks[4:6]
+        den_banks = banks[6:8]
+
+        last_num_banks = banks[0:2]
+
+        def sum_over_neighbours(bank, values, b, half):
+            for d in range(NEIGHBOURS):
+                nc.tensor.matmul(
+                    out=bank[:, P * b : P * (b + 1)], lhsT=values[:, d, P * half : P * (half + 1)],
+                    rhs=ident[:], is_transpose=True, start=(d == 0), stop=(d == NEIGHBOURS - 1),
+                )
+
+        def queries_and_keys(b):
+            y_bank, e_bank = banks[2 * (b % 2)], banks[2 * (b % 2) + 1]
+            product(y_bank, w1_codes, w1_plane, b)
+            product(e_bank, w2_codes, w2_plane, b)
+            nc.scalar.activation(out=y[b][:], in_=y_bank[:], func=ACT.Copy)
+            if b < 2:
+                nc.vector.tensor_copy(out=e[b][:], in_=e_bank[:])
+            else:
+                nc.scalar.copy(out=e[b][:], in_=e_bank[:])
+            nc.scalar.activation(out=yc[b][:], in_=y[b][:].indirect(cen_t[:]), func=ACT.Copy)
+
+        def differences(b):
+            for d in range(NEIGHBOURS):
+                nc.vector.tensor_tensor(out=diff[b][:, d, :], in0=e[b][:].indirect(pos_t[d][:]), in1=yc[b][:], op=ALU.subtract)
+
+        def distances(b):
+            nc.scalar.activation(out=dist[b][:], in_=diff[b][:], func=ACT.Abs)
+
+        def shift(b):
+            nc.vector.tensor_tensor(out=near2[b][:], in0=dist[b][:, 0, :], in1=dist[b][:, 1, :], op=ALU.min)
+            nc.vector.tensor_tensor(out=near3[b][:], in0=near2[b][:], in1=dist[b][:, 2, :], op=ALU.min)
+            nc.vector.tensor_tensor(
+                out=excess[b][:], in0=dist[b][:], in1=near3[b][:].unsqueeze(1).broadcast_to([P, NEIGHBOURS, V]), op=ALU.subtract
+            )
+
+        def weights(b):
+            nc.scalar.activation(out=weight[b][:], in_=excess[b][:], func=ACT.Exp, scale=-1.0)
+            for half in range(HALVES):
+                sum_over_neighbours(den_banks[half], weight[b], b, half)
+
+        def values(b):
+            bank = banks[b]
+            product(bank, w3_codes, w3_plane, b)
+            nc.scalar.copy(out=h[b][:], in_=bank[:])
+
+        def weighted_values(b):
+            for d in range(NEIGHBOURS):
+                nc.vector.tensor_tensor(out=term[b][:, d, :], in0=h[b][:].indirect(pos_t[d][:]), in1=weight[b][:, d, :], op=ALU.mult)
+            for half in range(HALVES):
+                sum_over_neighbours(num_banks[half], term[b], b, half)
+
+        def last_weighted_values(half):
+            b = BLOCKS - 1
+            cols = slice(P * half, P * (half + 1))
+            entries = slice(P // 16 * half, P // 16 * (half + 1))
+            for d in range(NEIGHBOURS):
+                nc.vector.tensor_tensor(out=term[b][:, d, cols], in0=h[b][:].indirect(pos_t[d][:, entries]), in1=weight[b][:, d, cols], op=ALU.mult)
+            sum_over_neighbours(last_num_banks[half], term[b], b, half)
+
+        for b in range(BLOCKS):
+            queries_and_keys(b)
+            differences(b)
+        distances(0)
+        distances(1)
+
+        w3_grouped = sbuf("w3_grouped", [P, H * PACK], BF16, tag="diff1")
+        nc.scalar.copy(
+            out=w3_grouped[:].rearrange("p (c i j) -> p c j i", i=4, j=PACK),
+            in_=w3_raw[:].rearrange("p j (c i) -> p c j i", i=4),
+        )
+        shift(0)
+        distances(2)
+        shift(1)
+        w3_codes = sbuf("w3_codes", [P, H], U32)
+        w3_plane = sbuf("w3_plane", [P, H], U8)
+        nc.vector.quantize_mx(out=w3_codes[:].bitcast(FP8X4), scales=w3_plane[:], in_=w3_grouped[:])
+        distances(3)
+        shift(2)
+        weights(0)
+        values(0)
+        shift(3)
+        weights(1)
+        values(1)
+        weighted_values(0)
+        weights(2)
+        weights(3)
+        values(2)
+        values(3)
+
+        w4_dealt = sbuf("w4_dealt", [P, N], U32, tag="excess1")
+        nc.scalar.copy(out=w4_dealt[:].rearrange("p (t m) -> p t m", t=PACK), in_=w4_codes[:].rearrange("p (m t) -> p t m", t=PACK))
+        w4_plane_dealt = sbuf("w4_plane_dealt", [P, N], U8)
+        nc.vector.tensor_copy(out=w4_plane_dealt[:].rearrange("p (t m) -> p t m", t=PACK), in_=w4_plane.rearrange("p (m t) -> p t m", t=PACK))
+
+        weighted_values(1)
+        weighted_values(2)
+        root = [sbuf("root%d" % half, [P, H], F32) for half in range(HALVES)]
+        inverse = [sbuf("inverse%d" % half, [P, H], F32) for half in range(HALVES)]
+        for half in range(HALVES):
+            nc.scalar.activation(out=root[half][:], in_=den_banks[half][:], func=ACT.Abs_reciprocal_sqrt)
+            nc.scalar.activation(out=inverse[half][:], in_=root[half][:], func=ACT.Square)
+        z_rows = [sbuf("z_rows%d" % half, [P, H], BF16) for half in range(HALVES)]
+        early = slice(0, H - P)
+        late = slice(H - P, H)
+        for half in range(HALVES):
+            last_weighted_values(half)
+            nc.vector.tensor_tensor(out=z_rows[half][:, early], in0=num_banks[half][:, early], in1=inverse[half][:, early], op=ALU.mult)
+
+        out_plane = sbuf("out_plane", [P, V], U8)
+        out_codes = sbuf("out_codes", [P, V], U32)
+        for half in range(HALVES):
+            cols = slice(P * half, P * (half + 1))
+            nc.vector.tensor_tensor(out=z_rows[half][:, late], in0=last_num_banks[half][:, late], in1=inverse[half][:, late], op=ALU.mult)
+            pairs = z_rows[half][:].bitcast(F32)
+            turn_bank = banks[2 + half]
+            for u in range(2):
+                nc.tensor.transpose(turn_bank[:, P * u : P * (u + 1)], pairs[:, u : H // 2 : 2], ident[:])
+            z_grouped = sbuf("z_grouped%d" % half, [P, P * PACK], BF16)
+            nc.scalar.copy(
+                out=z_grouped[:].bitcast(F32).rearrange("p (v u) -> p v u", u=2),
+                in_=turn_bank[:, 0 : 2 * P].rearrange("p (u v) -> p v u", u=2),
+            )
+            z_codes = sbuf("z_codes%d" % half, [P, P], U32)
+            z_plane = sbuf("z_plane%d" % half, [P, P], U8)
+            nc.vector.quantize_mx(out=z_codes[:].bitcast(FP8X4), scales=z_plane[:], in_=z_grouped[:])
+            out_bank = den_banks[half]
+            for t in range(PACK):
+                rows = slice(P * t, P * (t + 1))
+                nc.tensor.matmul_mx(
+                    out=out_bank[:, rows], lhsT=w4_dealt[:, rows].bitcast(FP8X4), lhsT_scale=w4_plane_dealt[:, rows],
+                    rhs=z_codes[:].bitcast(FP8X4), rhs_scale=z_plane[:], start=True, stop=True,
+                )
+            result = sbuf("result%d" % half, [P, PACK, P], F32)
+            nc.scalar.copy(out=result[:], in_=out_bank[:].rearrange("p (t v) -> p t v", t=PACK))
+            nc.sync.dma_start(out=out_0.rearrange("(p t) v -> p t v", t=PACK)[:, :, cols], in_=result[:])
+            out_grouped = sbuf("out_grouped%d" % half, [P, P * PACK], BF16)
+            nc.vector.tensor_copy(
+                out=out_grouped[:].rearrange("p (v t) -> p v t", t=PACK), in_=result[:].rearrange("p t v -> p v t")
+            )
+            nc.vector.quantize_mx(out=out_codes[:, cols].bitcast(FP8X4), scales=out_plane[:, cols], in_=out_grouped[:])
+
+        nc.sync.dma_start(out=out_1[0].rearrange("p n t -> p (n t)").bitcast(I32), in_=out_codes[:].bitcast(I32))
+        for q in range(QUADRANTS):
+            nc.scalar.dma_start(out=out_2[0][4 * q : 4 * q + 4, :].bitcast(I32), in_=out_plane[32 * q : 32 * q + 4, :].bitcast(I32))

@@ -40,9 +40,9 @@ def tile_picked_zpt_lap_po_kernel(
         def load_words(tile, words):
             nc.sync.dma_start(out=tile[:].bitcast(I32), in_=words[0].rearrange("p n t -> p (n t)").bitcast(I32))
 
-        def load_scales(queue, plane, scales):
+        def load_scales(plane, scales):
             for q in range(QUADRANTS):
-                queue.dma_start(out=plane[32 * q : 32 * q + 4, :].bitcast(I32), in_=scales[0][4 * q : 4 * q + 4, :].bitcast(I32))
+                nc.sync.dma_start(out=plane[32 * q : 32 * q + 4, :].bitcast(I32), in_=scales[0][4 * q : 4 * q + 4, :].bitcast(I32))
 
         def load_list(name, dram, entries):
             tile = keep.tile([P, entries // 16], U16, name=name)
@@ -51,38 +51,37 @@ def tile_picked_zpt_lap_po_kernel(
 
         banks = [psum.tile([P, 512], F32, name="bank%d" % b) for b in range(8)]
 
-        x_plane = sbuf("x_plane", [P, T], U8, tag="x_plane_bytes")
+        x_plane = sbuf("x_plane", [P, T], U8)
         w_planes = sbuf("w_planes", [P, 3 * N], U8)
-        nc.vector.memset(x_plane[:].bitcast(I32), 0)
-        nc.gpsimd.memset(w_planes[:].bitcast(I32), 0)
+        nc.gpsimd.memset(x_plane[:].bitcast(I32), 0)
+        nc.vector.memset(w_planes[:].bitcast(I32), 0)
         w1_plane, w2_plane, w4_plane = (w_planes[:, j * N : (j + 1) * N] for j in range(3))
 
         offs_t = load_list("offs_t", offs, S)
         cen_t = load_list("cen_t", cen, V)
-        pos_t = [load_list("pos%d_t" % d, pos, V) for d, pos in enumerate((pos1, pos2, pos3))]
-        x_codes = sbuf("x_codes", [P, T], U32, tag="x_codes_bytes")
+        load_scales(x_plane[:], x_scales)
+        x_codes = sbuf("x_codes", [P, T], U32)
         load_words(x_codes, x_words)
         w1_codes = sbuf("w1_codes", [P, N], U32)
         load_words(w1_codes, w1_words)
+        load_scales(w1_plane, w1_scales)
         w2_codes = sbuf("w2_codes", [P, N], U32)
         load_words(w2_codes, w2_words)
-        load_scales(nc.sync, x_plane[:], x_scales)
-        load_scales(nc.sync, w1_plane, w1_scales)
-        load_scales(nc.sync, w2_plane, w2_scales)
-        load_scales(nc.gpsimd, w4_plane, w4_scales)
+        load_scales(w2_plane, w2_scales)
+        pos_t = [load_list("pos%d_t" % d, pos, V) for d, pos in enumerate((pos1, pos2, pos3))]
+        w3_raw = sbuf("w3_raw", [P, PACK, H], F32)
+        nc.sync.dma_start(out=w3_raw[:], in_=w3.rearrange("(p j) c -> p j c", j=PACK))
+        w4_codes = sbuf("w4_codes", [P, N], U32)
+        load_words(w4_codes, w4_words)
+        load_scales(w4_plane, w4_scales)
 
         ident = sbuf("ident", [P, P], F32)
         make_identity(nc, ident[:])
 
-        xq_codes = sbuf("xq_codes", [P, S], U32)
-        nc.vector.tensor_copy(out=xq_codes[:], in_=x_codes[:].indirect(offs_t[:]))
         xq_plane = sbuf("xq_plane", [P, S], U8)
         nc.vector.tensor_copy(out=xq_plane[:], in_=x_plane[:].indirect(offs_t[:]))
-
-        w3_raw = sbuf("w3_raw", [P, PACK, H], F32, tag="x_codes_bytes")
-        nc.sync.dma_start(out=w3_raw[:], in_=w3.rearrange("(p j) c -> p j c", j=PACK))
-        w4_codes = sbuf("w4_codes", [P, N], U32, tag="x_plane_bytes")
-        load_words(w4_codes, w4_words)
+        xq_codes = sbuf("xq_codes", [P, S], U32)
+        nc.vector.tensor_copy(out=xq_codes[:], in_=x_codes[:].indirect(offs_t[:]))
 
         def product(bank, codes, plane, b):
             cols = slice(P * b, P * (b + 1))
@@ -115,19 +114,27 @@ def tile_picked_zpt_lap_po_kernel(
                 )
 
         def queries_and_keys(b):
-            y_bank, e_bank = banks[2 * (b % 2)], banks[2 * (b % 2) + 1]
+            y_bank, e_bank = banks[2 * (b % 2) + b // 2], banks[2 * (b % 2) + 1 - b // 2]
             product(y_bank, w1_codes, w1_plane, b)
             product(e_bank, w2_codes, w2_plane, b)
             nc.scalar.activation(out=y[b][:], in_=y_bank[:], func=ACT.Copy)
-            if b < 2:
+            if b == 0:
                 nc.vector.tensor_copy(out=e[b][:], in_=e_bank[:])
             else:
                 nc.scalar.copy(out=e[b][:], in_=e_bank[:])
             nc.scalar.activation(out=yc[b][:], in_=y[b][:].indirect(cen_t[:]), func=ACT.Copy)
 
         def differences(b):
-            for d in range(NEIGHBOURS):
-                nc.vector.tensor_tensor(out=diff[b][:, d, :], in0=e[b][:].indirect(pos_t[d][:]), in1=yc[b][:], op=ALU.subtract)
+            if b < BLOCKS - 1:
+                for d in range(NEIGHBOURS):
+                    nc.vector.tensor_tensor(out=diff[b][:, d, :], in0=e[b][:].indirect(pos_t[d][:]), in1=yc[b][:], op=ALU.subtract)
+            else:
+                keys = sbuf("keys", [P, NEIGHBOURS, V], F32)
+                for d in range(NEIGHBOURS):
+                    nc.scalar.activation(out=keys[:, d, :], in_=e[b][:].indirect(pos_t[d][:]), func=ACT.Copy)
+                nc.vector.tensor_tensor(
+                    out=diff[b][:], in0=keys[:], in1=yc[b][:].unsqueeze(1).broadcast_to([P, NEIGHBOURS, V]), op=ALU.subtract
+                )
 
         def distances(b):
             nc.scalar.activation(out=dist[b][:], in_=diff[b][:], func=ACT.Abs)
@@ -165,46 +172,36 @@ def tile_picked_zpt_lap_po_kernel(
 
         for b in range(BLOCKS):
             queries_and_keys(b)
+        for b in range(BLOCKS - 1):
             differences(b)
-        distances(0)
-        distances(1)
+            distances(b)
 
-        w3_grouped = sbuf("w3_grouped", [P, H * PACK], BF16, tag="diff1")
+        w3_grouped = sbuf("w3_grouped", [P, H * PACK], BF16, tag="diff0")
         nc.scalar.copy(
             out=w3_grouped[:].rearrange("p (c i j) -> p c j i", i=4, j=PACK),
             in_=w3_raw[:].rearrange("p j (c i) -> p c j i", i=4),
         )
-        shift(0)
-        distances(2)
-        shift(1)
         w3_codes = sbuf("w3_codes", [P, H], U32)
         w3_plane = sbuf("w3_plane", [P, H], U8)
         nc.vector.quantize_mx(out=w3_codes[:].bitcast(FP8X4), scales=w3_plane[:], in_=w3_grouped[:])
-        distances(3)
-        shift(2)
-        weights(0)
-        values(0)
-        shift(3)
-        weights(1)
-        values(1)
-        weighted_values(0)
-        weights(2)
-        weights(3)
-        values(2)
-        values(3)
-
-        w4_dealt = sbuf("w4_dealt", [P, N], U32, tag="excess1")
-        nc.scalar.copy(out=w4_dealt[:].rearrange("p (t m) -> p t m", t=PACK), in_=w4_codes[:].rearrange("p (m t) -> p t m", t=PACK))
         w4_plane_dealt = sbuf("w4_plane_dealt", [P, N], U8)
         nc.vector.tensor_copy(out=w4_plane_dealt[:].rearrange("p (t m) -> p t m", t=PACK), in_=w4_plane.rearrange("p (m t) -> p t m", t=PACK))
 
-        weighted_values(1)
-        weighted_values(2)
+        differences(BLOCKS - 1)
+        distances(BLOCKS - 1)
+        for b in range(BLOCKS):
+            shift(b)
+            values(b)
+            weights(b)
+        for b in range(BLOCKS - 1):
+            weighted_values(b)
         root = [sbuf("root%d" % half, [P, H], F32) for half in range(HALVES)]
         inverse = [sbuf("inverse%d" % half, [P, H], F32) for half in range(HALVES)]
         for half in range(HALVES):
             nc.scalar.activation(out=root[half][:], in_=den_banks[half][:], func=ACT.Abs_reciprocal_sqrt)
             nc.scalar.activation(out=inverse[half][:], in_=root[half][:], func=ACT.Square)
+        w4_dealt = sbuf("w4_dealt", [P, N], U32, tag="root0")
+        nc.scalar.copy(out=w4_dealt[:].rearrange("p (t m) -> p t m", t=PACK), in_=w4_codes[:].rearrange("p (m t) -> p t m", t=PACK))
         z_rows = [sbuf("z_rows%d" % half, [P, H], BF16) for half in range(HALVES)]
         early = slice(0, H - P)
         late = slice(H - P, H)
@@ -247,4 +244,4 @@ def tile_picked_zpt_lap_po_kernel(
 
         nc.sync.dma_start(out=out_1[0].rearrange("p n t -> p (n t)").bitcast(I32), in_=out_codes[:].bitcast(I32))
         for q in range(QUADRANTS):
-            nc.scalar.dma_start(out=out_2[0][4 * q : 4 * q + 4, :].bitcast(I32), in_=out_plane[32 * q : 32 * q + 4, :].bitcast(I32))
+            (nc.scalar if q % 2 else nc.sync).dma_start(out=out_2[0][4 * q : 4 * q + 4, :].bitcast(I32), in_=out_plane[32 * q : 32 * q + 4, :].bitcast(I32))

@@ -18,10 +18,17 @@ ALU = mybir.AluOpType
 
 P = 128
 PACK = 4
-BLOCKS = H // P
-HALVES = V // P
-NEIGHBOURS = 3
+BANK = 512
+LIST_ROWS = 16
 QUADRANTS = 4
+LINE = 4
+NEIGHBOURS = 3
+BLOCKS = H // P
+LAST = BLOCKS - 1
+HALVES = V // P
+
+CENTRES_ON_VECTOR = 2
+W3_COLUMNS_ON_SCALAR = H // 2
 
 
 def tile_picked_zpt_lap_po_kernel(
@@ -34,22 +41,31 @@ def tile_picked_zpt_lap_po_kernel(
         keep = ctx.enter_context(tc.tile_pool(name="keep", bufs=1))
         psum = ctx.enter_context(tc.psum_pool(name="psum", bufs=1))
 
-        def sbuf(name, shape, dtype, tag=None):
-            return keep.tile(shape, dtype, name=name, tag=tag or name, align_bytes=64)
+        def sbuf(name, shape, dtype, reuses=None):
+            return keep.tile(shape, dtype, name=name, tag=reuses or name, align_bytes=64)
 
-        def load_words(tile, words):
+        def load_words(name, words, columns):
+            tile = sbuf(name, [P, columns], U32)
             nc.sync.dma_start(out=tile[:].bitcast(I32), in_=words[0].rearrange("p n t -> p (n t)").bitcast(I32))
+            return tile
 
         def load_scales(plane, scales):
             for q in range(QUADRANTS):
                 nc.sync.dma_start(out=plane[32 * q : 32 * q + 4, :].bitcast(I32), in_=scales[0][4 * q : 4 * q + 4, :].bitcast(I32))
 
         def load_list(name, dram, entries):
-            tile = keep.tile([P, entries // 16], U16, name=name)
+            tile = keep.tile([P, entries // LIST_ROWS], U16, name=name)
             nc.sync.dma_start(tile[:], dram)
             return tile
 
-        banks = [psum.tile([P, 512], F32, name="bank%d" % b) for b in range(8)]
+        def entries(tile, columns):
+            return tile[:, columns.start // LIST_ROWS : columns.stop // LIST_ROWS]
+
+        banks = [psum.tile([P, BANK], F32, name="bank%d" % b) for b in range(8)]
+        num_banks = banks[4:6]
+        den_banks = banks[6:8]
+        last_num_banks = banks[0:2]
+        turn_banks = banks[2:4]
 
         x_plane = sbuf("x_plane", [P, T], U8)
         w_planes = sbuf("w_planes", [P, 3 * N], U8)
@@ -59,82 +75,86 @@ def tile_picked_zpt_lap_po_kernel(
 
         offs_t = load_list("offs_t", offs, S)
         cen_t = load_list("cen_t", cen, V)
+        pos1_t = load_list("pos1_t", pos1, V)
         load_scales(x_plane[:], x_scales)
-        x_codes = sbuf("x_codes", [P, T], U32)
-        load_words(x_codes, x_words)
-        w1_codes = sbuf("w1_codes", [P, N], U32)
-        load_words(w1_codes, w1_words)
+        x_codes = load_words("x_codes", x_words, T)
         load_scales(w1_plane, w1_scales)
-        w2_codes = sbuf("w2_codes", [P, N], U32)
-        load_words(w2_codes, w2_words)
+        w1_codes = load_words("w1_codes", w1_words, N)
+        w2_codes = load_words("w2_codes", w2_words, N)
         load_scales(w2_plane, w2_scales)
-        pos_t = [load_list("pos%d_t" % d, pos, V) for d, pos in enumerate((pos1, pos2, pos3))]
+        pos_t = [pos1_t, load_list("pos2_t", pos2, V), load_list("pos3_t", pos3, V)]
         w3_raw = sbuf("w3_raw", [P, PACK, H], F32)
-        nc.sync.dma_start(out=w3_raw[:], in_=w3.rearrange("(p j) c -> p j c", j=PACK))
-        w4_codes = sbuf("w4_codes", [P, N], U32)
-        load_words(w4_codes, w4_words)
+        nc.sync.dma_start(out=w3_raw[:], in_=w3.rearrange("(p t) c -> p t c", t=PACK))
+        w4_codes = load_words("w4_codes", w4_words, N)
         load_scales(w4_plane, w4_scales)
 
         ident = sbuf("ident", [P, P], F32)
         make_identity(nc, ident[:])
 
+        point_parts = (slice(0, S // 2), slice(S // 2, S))
         xq_plane = sbuf("xq_plane", [P, S], U8)
         nc.vector.tensor_copy(out=xq_plane[:], in_=x_plane[:].indirect(offs_t[:]))
         xq_codes = sbuf("xq_codes", [P, S], U32)
-        nc.vector.tensor_copy(out=xq_codes[:], in_=x_codes[:].indirect(offs_t[:]))
+        for points in point_parts:
+            nc.vector.tensor_copy(out=xq_codes[:, points], in_=x_codes[:].indirect(entries(offs_t, points)))
 
-        def product(bank, codes, plane, b):
-            cols = slice(P * b, P * (b + 1))
+        def product(bank, codes, plane, b, points=slice(0, S)):
+            features = slice(P * b, P * (b + 1))
             nc.tensor.matmul_mx(
-                out=bank[:], lhsT=codes[:, cols].bitcast(FP8X4), lhsT_scale=plane[:, cols],
-                rhs=xq_codes[:].bitcast(FP8X4), rhs_scale=xq_plane[:], start=True, stop=True,
+                out=bank[:, points], lhsT=codes[:, features].bitcast(FP8X4), lhsT_scale=plane[:, features],
+                rhs=xq_codes[:, points].bitcast(FP8X4), rhs_scale=xq_plane[:, points], start=True, stop=True,
             )
 
-        y = [sbuf("y%d" % b, [P, S], F32) for b in range(BLOCKS)]
-        e = [sbuf("e%d" % b, [P, S], F32) for b in range(BLOCKS)]
-        h = [sbuf("h%d" % b, [P, S], F32) for b in range(BLOCKS)]
-        yc = [sbuf("yc%d" % b, [P, V], F32) for b in range(BLOCKS)]
-        diff = [sbuf("diff%d" % b, [P, NEIGHBOURS, V], F32) for b in range(BLOCKS)]
-        dist = [sbuf("dist%d" % b, [P, NEIGHBOURS, V], F32) for b in range(BLOCKS)]
-        near2 = [sbuf("near2_%d" % b, [P, V], F32) for b in range(BLOCKS)]
-        near3 = [sbuf("near3_%d" % b, [P, V], F32) for b in range(BLOCKS)]
-        excess = [sbuf("excess%d" % b, [P, NEIGHBOURS, V], F32) for b in range(BLOCKS)]
-        weight = [sbuf("weight%d" % b, [P, NEIGHBOURS, V], F32) for b in range(BLOCKS)]
-        term = [sbuf("term%d" % b, [P, NEIGHBOURS, V], F32) for b in range(BLOCKS)]
-        num_banks = banks[4:6]
-        den_banks = banks[6:8]
+        def per_block(name, shape):
+            return [sbuf("%s%d" % (name, b), shape, F32) for b in range(BLOCKS)]
 
-        last_num_banks = banks[0:2]
+        y = per_block("y", [P, S])
+        e = per_block("e", [P, S])
+        h = per_block("h", [P, S])
+        yc = per_block("yc", [P, V])
+        diff = per_block("diff", [P, NEIGHBOURS, V])
+        dist = per_block("dist", [P, NEIGHBOURS, V])
+        near2 = per_block("near2_", [P, V])
+        near3 = per_block("near3_", [P, V])
+        excess = per_block("excess", [P, NEIGHBOURS, V])
+        weight = per_block("weight", [P, NEIGHBOURS, V])
+        term = per_block("term", [P, NEIGHBOURS, V])
 
-        def sum_over_neighbours(bank, values, b, half):
+        def for_each_neighbour(row):
+            return row[:].unsqueeze(1).broadcast_to([P, NEIGHBOURS, V])
+
+        def sum_over_neighbours(bank, summands, b, half):
             for d in range(NEIGHBOURS):
                 nc.tensor.matmul(
-                    out=bank[:, P * b : P * (b + 1)], lhsT=values[:, d, P * half : P * (half + 1)],
+                    out=bank[:, P * b : P * (b + 1)], lhsT=summands[:, d, P * half : P * (half + 1)],
                     rhs=ident[:], is_transpose=True, start=(d == 0), stop=(d == NEIGHBOURS - 1),
                 )
 
         def queries_and_keys(b):
             y_bank, e_bank = banks[2 * (b % 2) + b // 2], banks[2 * (b % 2) + 1 - b // 2]
-            product(y_bank, w1_codes, w1_plane, b)
-            product(e_bank, w2_codes, w2_plane, b)
-            nc.scalar.activation(out=y[b][:], in_=y_bank[:], func=ACT.Copy)
             if b == 0:
-                nc.vector.tensor_copy(out=e[b][:], in_=e_bank[:])
+                for bank, points in zip((num_banks[0], y_bank), point_parts):
+                    product(bank, w1_codes, w1_plane, b, points)
+                    nc.scalar.activation(out=y[b][:, points], in_=bank[:, points], func=ACT.Copy)
             else:
-                nc.scalar.copy(out=e[b][:], in_=e_bank[:])
-            nc.scalar.activation(out=yc[b][:], in_=y[b][:].indirect(cen_t[:]), func=ACT.Copy)
+                product(y_bank, w1_codes, w1_plane, b)
+                nc.scalar.activation(out=y[b][:], in_=y_bank[:], func=ACT.Copy)
+            product(e_bank, w2_codes, w2_plane, b)
+            nc.scalar.copy(out=e[b][:], in_=e_bank[:])
+            if b < CENTRES_ON_VECTOR:
+                nc.vector.tensor_copy(out=yc[b][:], in_=y[b][:].indirect(cen_t[:]))
+            else:
+                nc.scalar.activation(out=yc[b][:], in_=y[b][:].indirect(cen_t[:]), func=ACT.Copy)
 
         def differences(b):
-            if b < BLOCKS - 1:
+            if b < LAST:
                 for d in range(NEIGHBOURS):
                     nc.vector.tensor_tensor(out=diff[b][:, d, :], in0=e[b][:].indirect(pos_t[d][:]), in1=yc[b][:], op=ALU.subtract)
             else:
                 keys = sbuf("keys", [P, NEIGHBOURS, V], F32)
                 for d in range(NEIGHBOURS):
                     nc.scalar.activation(out=keys[:, d, :], in_=e[b][:].indirect(pos_t[d][:]), func=ACT.Copy)
-                nc.vector.tensor_tensor(
-                    out=diff[b][:], in0=keys[:], in1=yc[b][:].unsqueeze(1).broadcast_to([P, NEIGHBOURS, V]), op=ALU.subtract
-                )
+                nc.vector.tensor_tensor(out=diff[b][:], in0=keys[:], in1=for_each_neighbour(yc[b]), op=ALU.subtract)
 
         def distances(b):
             nc.scalar.activation(out=dist[b][:], in_=diff[b][:], func=ACT.Abs)
@@ -142,9 +162,7 @@ def tile_picked_zpt_lap_po_kernel(
         def shift(b):
             nc.vector.tensor_tensor(out=near2[b][:], in0=dist[b][:, 0, :], in1=dist[b][:, 1, :], op=ALU.min)
             nc.vector.tensor_tensor(out=near3[b][:], in0=near2[b][:], in1=dist[b][:, 2, :], op=ALU.min)
-            nc.vector.tensor_tensor(
-                out=excess[b][:], in0=dist[b][:], in1=near3[b][:].unsqueeze(1).broadcast_to([P, NEIGHBOURS, V]), op=ALU.subtract
-            )
+            nc.vector.tensor_tensor(out=excess[b][:], in0=dist[b][:], in1=for_each_neighbour(near3[b]), op=ALU.subtract)
 
         def weights(b):
             nc.scalar.activation(out=weight[b][:], in_=excess[b][:], func=ACT.Exp, scale=-1.0)
@@ -152,9 +170,8 @@ def tile_picked_zpt_lap_po_kernel(
                 sum_over_neighbours(den_banks[half], weight[b], b, half)
 
         def values(b):
-            bank = banks[b]
-            product(bank, w3_codes, w3_plane, b)
-            nc.scalar.copy(out=h[b][:], in_=bank[:])
+            product(banks[b], w3_codes, w3_plane, b)
+            nc.scalar.copy(out=h[b][:], in_=banks[b][:])
 
         def weighted_values(b):
             for d in range(NEIGHBOURS):
@@ -162,86 +179,108 @@ def tile_picked_zpt_lap_po_kernel(
             for half in range(HALVES):
                 sum_over_neighbours(num_banks[half], term[b], b, half)
 
-        def last_weighted_values(half):
-            b = BLOCKS - 1
-            cols = slice(P * half, P * (half + 1))
-            entries = slice(P // 16 * half, P // 16 * (half + 1))
-            for d in range(NEIGHBOURS):
-                nc.vector.tensor_tensor(out=term[b][:, d, cols], in0=h[b][:].indirect(pos_t[d][:, entries]), in1=weight[b][:, d, cols], op=ALU.mult)
-            sum_over_neighbours(last_num_banks[half], term[b], b, half)
-
         for b in range(BLOCKS):
             queries_and_keys(b)
-        for b in range(BLOCKS - 1):
             differences(b)
-            distances(b)
+        distances(0)
 
-        w3_grouped = sbuf("w3_grouped", [P, H * PACK], BF16, tag="diff0")
-        nc.scalar.copy(
-            out=w3_grouped[:].rearrange("p (c i j) -> p c j i", i=4, j=PACK),
-            in_=w3_raw[:].rearrange("p j (c i) -> p c j i", i=4),
-        )
+        w3_grouped = sbuf("w3_grouped", [P, H * PACK], BF16, reuses="diff0")
         w3_codes = sbuf("w3_codes", [P, H], U32)
         w3_plane = sbuf("w3_plane", [P, H], U8)
+        grouped_lines = w3_grouped[:].rearrange("p (c i t) -> p c t i", i=LINE, t=PACK)
+        raw_lines = w3_raw[:].rearrange("p t (c i) -> p c t i", i=LINE)
+        split = W3_COLUMNS_ON_SCALAR // LINE
+        nc.scalar.copy(out=grouped_lines[:, 0:split], in_=raw_lines[:, 0:split])
+        nc.vector.tensor_copy(out=grouped_lines[:, split : H // LINE], in_=raw_lines[:, split : H // LINE])
         nc.vector.quantize_mx(out=w3_codes[:].bitcast(FP8X4), scales=w3_plane[:], in_=w3_grouped[:])
+
         w4_plane_dealt = sbuf("w4_plane_dealt", [P, N], U8)
         nc.vector.tensor_copy(out=w4_plane_dealt[:].rearrange("p (t m) -> p t m", t=PACK), in_=w4_plane.rearrange("p (m t) -> p t m", t=PACK))
 
-        differences(BLOCKS - 1)
-        distances(BLOCKS - 1)
+        for b in range(1, BLOCKS):
+            distances(b)
+
         for b in range(BLOCKS):
             shift(b)
             values(b)
             weights(b)
-        for b in range(BLOCKS - 1):
+        for b in range(LAST):
             weighted_values(b)
+
         root = [sbuf("root%d" % half, [P, H], F32) for half in range(HALVES)]
         inverse = [sbuf("inverse%d" % half, [P, H], F32) for half in range(HALVES)]
         for half in range(HALVES):
             nc.scalar.activation(out=root[half][:], in_=den_banks[half][:], func=ACT.Abs_reciprocal_sqrt)
             nc.scalar.activation(out=inverse[half][:], in_=root[half][:], func=ACT.Square)
-        w4_dealt = sbuf("w4_dealt", [P, N], U32, tag="root0")
-        nc.scalar.copy(out=w4_dealt[:].rearrange("p (t m) -> p t m", t=PACK), in_=w4_codes[:].rearrange("p (m t) -> p t m", t=PACK))
+
+        centre_halves = [slice(P * half, P * (half + 1)) for half in range(HALVES)]
+        picked = sbuf("picked", [P, NEIGHBOURS, P], F32, reuses="excess%d" % LAST)
+        for d in range(NEIGHBOURS):
+            nc.scalar.activation(out=picked[:, d, :], in_=h[LAST][:].indirect(entries(pos_t[d], centre_halves[1])), func=ACT.Copy)
+
+        w4_dealt = sbuf("w4_dealt", [P, N], U32, reuses="root1")
+        nc.scalar.copy(out=w4_dealt[:].rearrange("p (t m) -> p m t", t=PACK), in_=w4_codes[:].rearrange("p (m t) -> p m t", t=PACK))
+
         z_rows = [sbuf("z_rows%d" % half, [P, H], BF16) for half in range(HALVES)]
-        early = slice(0, H - P)
-        late = slice(H - P, H)
-        for half in range(HALVES):
-            last_weighted_values(half)
-            nc.vector.tensor_tensor(out=z_rows[half][:, early], in0=num_banks[half][:, early], in1=inverse[half][:, early], op=ALU.mult)
+
+        def divide(half, numerators, features):
+            quads = slice(features.start // PACK, features.stop // PACK)
+            nc.vector.tensor_tensor(
+                out=z_rows[half][:].rearrange("v (u p j) -> v p u j", u=2, j=2)[:, quads],
+                in0=numerators[:].rearrange("v (p u j) -> v p u j", u=2, j=2)[:, quads],
+                in1=inverse[half][:].rearrange("v (p u j) -> v p u j", u=2, j=2)[:, quads],
+                op=ALU.mult,
+            )
+
+        for half, centres in enumerate(centre_halves):
+            if half == 0:
+                for d in range(NEIGHBOURS):
+                    nc.vector.tensor_tensor(
+                        out=term[LAST][:, d, centres], in0=h[LAST][:].indirect(entries(pos_t[d], centres)),
+                        in1=weight[LAST][:, d, centres], op=ALU.mult,
+                    )
+            else:
+                nc.vector.tensor_tensor(out=term[LAST][:, :, centres], in0=picked[:], in1=weight[LAST][:, :, centres], op=ALU.mult)
+            sum_over_neighbours(last_num_banks[half], term[LAST], LAST, half)
+            divide(half, num_banks[half], slice(0, P * LAST))
 
         out_plane = sbuf("out_plane", [P, V], U8)
         out_codes = sbuf("out_codes", [P, V], U32)
-        for half in range(HALVES):
-            cols = slice(P * half, P * (half + 1))
-            nc.vector.tensor_tensor(out=z_rows[half][:, late], in0=last_num_banks[half][:, late], in1=inverse[half][:, late], op=ALU.mult)
+        for half, centres in enumerate(centre_halves):
+            divide(half, last_num_banks[half], slice(P * LAST, H))
+
             pairs = z_rows[half][:].bitcast(F32)
-            turn_bank = banks[2 + half]
             for u in range(2):
-                nc.tensor.transpose(turn_bank[:, P * u : P * (u + 1)], pairs[:, u : H // 2 : 2], ident[:])
+                nc.tensor.transpose(turn_banks[half][:, P * u : P * (u + 1)], pairs[:, P * u : P * (u + 1)], ident[:])
             z_grouped = sbuf("z_grouped%d" % half, [P, P * PACK], BF16)
             nc.scalar.copy(
                 out=z_grouped[:].bitcast(F32).rearrange("p (v u) -> p v u", u=2),
-                in_=turn_bank[:, 0 : 2 * P].rearrange("p (u v) -> p v u", u=2),
+                in_=turn_banks[half][:, 0 : 2 * P].rearrange("p (u v) -> p v u", u=2),
             )
             z_codes = sbuf("z_codes%d" % half, [P, P], U32)
             z_plane = sbuf("z_plane%d" % half, [P, P], U8)
             nc.vector.quantize_mx(out=z_codes[:].bitcast(FP8X4), scales=z_plane[:], in_=z_grouped[:])
-            out_bank = den_banks[half]
+
+            out_banks = (den_banks[half], num_banks[half])
             for t in range(PACK):
                 rows = slice(P * t, P * (t + 1))
                 nc.tensor.matmul_mx(
-                    out=out_bank[:, rows], lhsT=w4_dealt[:, rows].bitcast(FP8X4), lhsT_scale=w4_plane_dealt[:, rows],
+                    out=out_banks[t // 2][:, P * (t % 2) : P * (t % 2 + 1)],
+                    lhsT=w4_dealt[:, rows].bitcast(FP8X4), lhsT_scale=w4_plane_dealt[:, rows],
                     rhs=z_codes[:].bitcast(FP8X4), rhs_scale=z_plane[:], start=True, stop=True,
                 )
             result = sbuf("result%d" % half, [P, PACK, P], F32)
-            nc.scalar.copy(out=result[:], in_=out_bank[:].rearrange("p (t v) -> p t v", t=PACK))
-            nc.sync.dma_start(out=out_0.rearrange("(p t) v -> p t v", t=PACK)[:, :, cols], in_=result[:])
+            for j, bank in enumerate(out_banks):
+                nc.scalar.copy(out=result[:, 2 * j : 2 * j + 2, :], in_=bank[:, 0 : 2 * P].rearrange("p (t v) -> p t v", t=2))
+            nc.sync.dma_start(out=out_0.rearrange("(p t) v -> p t v", t=PACK)[:, :, centres], in_=result[:])
+
             out_grouped = sbuf("out_grouped%d" % half, [P, P * PACK], BF16)
             nc.vector.tensor_copy(
-                out=out_grouped[:].rearrange("p (v t) -> p v t", t=PACK), in_=result[:].rearrange("p t v -> p v t")
+                out=out_grouped[:].rearrange("p (c i t) -> p c t i", i=LINE, t=PACK), in_=result[:].rearrange("p t (c i) -> p c t i", i=LINE)
             )
-            nc.vector.quantize_mx(out=out_codes[:, cols].bitcast(FP8X4), scales=out_plane[:, cols], in_=out_grouped[:])
+            nc.vector.quantize_mx(out=out_codes[:, centres].bitcast(FP8X4), scales=out_plane[:, centres], in_=out_grouped[:])
+            nc.sync.dma_start(out=out_1[0].rearrange("p n t -> p (n t)").bitcast(I32)[:, centres], in_=out_codes[:, centres].bitcast(I32))
 
-        nc.sync.dma_start(out=out_1[0].rearrange("p n t -> p (n t)").bitcast(I32), in_=out_codes[:].bitcast(I32))
         for q in range(QUADRANTS):
-            (nc.scalar if q % 2 else nc.sync).dma_start(out=out_2[0][4 * q : 4 * q + 4, :].bitcast(I32), in_=out_plane[32 * q : 32 * q + 4, :].bitcast(I32))
+            queue = nc.scalar if q % 2 else nc.sync
+            queue.dma_start(out=out_2[0][4 * q : 4 * q + 4, :].bitcast(I32), in_=out_plane[32 * q : 32 * q + 4, :].bitcast(I32))

from contextlib import ExitStack

import concourse.mybir as mybir
from concourse.masks import make_identity

K, T, S, V, H, N = 512, 2048, 512, 256, 512, 512
FLOPS = 2 * K * S * (N + N + H) + 2 * H * N * V

F32 = mybir.dt.float32
BF16 = mybir.dt.bfloat16
I32 = mybir.dt.int32
U32 = mybir.dt.uint32
U16 = mybir.dt.uint16
U8 = mybir.dt.uint8
FP8X4 = mybir.dt.float8_e4m3fn_x4
ACT = mybir.ActivationFunctionType
ALU = mybir.AluOpType

P = 128
PACK = 4
BANK = 512
LIST_ROWS = 16
QUADRANTS = 4
LINE = 4
NEIGHBOURS = 3
BLOCKS = H // P
LAST = BLOCKS - 1
HALVES = V // P

CENTRES_ON_VECTOR = 2
W3_COLUMNS_ON_SCALAR = H // 2


def tile_picked_zpt_lap_po_kernel(
    tc, x_words, x_scales, w1_words, w1_scales, w2_words, w2_scales, w3, w4_words, w4_scales,
    offs, cen, pos1, pos2, pos3, out_0, out_1, out_2,
):
    nc = tc.nc

    with ExitStack() as ctx:
        keep = ctx.enter_context(tc.tile_pool(name="keep", bufs=1))
        psum = ctx.enter_context(tc.psum_pool(name="psum", bufs=1))

        def sbuf(name, shape, dtype, reuses=None):
            return keep.tile(shape, dtype, name=name, tag=reuses or name, align_bytes=64)

        def load_words(name, words, columns):
            tile = sbuf(name, [P, columns], U32)
            nc.sync.dma_start(out=tile[:].bitcast(I32), in_=words[0].rearrange("p n t -> p (n t)").bitcast(I32))
            return tile

        def load_scales(plane, scales):
            for q in range(QUADRANTS):
                nc.sync.dma_start(out=plane[32 * q : 32 * q + 4, :].bitcast(I32), in_=scales[0][4 * q : 4 * q + 4, :].bitcast(I32))

        def load_list(name, dram, entries):
            tile = keep.tile([P, entries // LIST_ROWS], U16, name=name)
            nc.sync.dma_start(tile[:], dram)
            return tile

        def entries(tile, columns):
            return tile[:, columns.start // LIST_ROWS : columns.stop // LIST_ROWS]

        banks = [psum.tile([P, BANK], F32, name="bank%d" % b) for b in range(8)]
        num_banks = banks[4:6]
        den_banks = banks[6:8]
        last_num_banks = banks[0:2]
        turn_banks = banks[2:4]

        x_plane = sbuf("x_plane", [P, T], U8)
        w_planes = sbuf("w_planes", [P, 3 * N], U8)
        nc.gpsimd.memset(x_plane[:].bitcast(I32), 0)
        nc.vector.memset(w_planes[:].bitcast(I32), 0)
        w1_plane, w2_plane, w4_plane = (w_planes[:, j * N : (j + 1) * N] for j in range(3))

        offs_t = load_list("offs_t", offs, S)
        cen_t = load_list("cen_t", cen, V)
        pos1_t = load_list("pos1_t", pos1, V)
        load_scales(x_plane[:], x_scales)
        x_codes = load_words("x_codes", x_words, T)
        load_scales(w1_plane, w1_scales)
        w1_codes = load_words("w1_codes", w1_words, N)
        w2_codes = load_words("w2_codes", w2_words, N)
        load_scales(w2_plane, w2_scales)
        pos_t = [pos1_t, load_list("pos2_t", pos2, V), load_list("pos3_t", pos3, V)]
        w3_raw = sbuf("w3_raw", [P, PACK, H], F32)
        nc.sync.dma_start(out=w3_raw[:], in_=w3.rearrange("(p t) c -> p t c", t=PACK))
        w4_codes = load_words("w4_codes", w4_words, N)
        load_scales(w4_plane, w4_scales)

        ident = sbuf("ident", [P, P], F32)
        make_identity(nc, ident[:])

        point_parts = (slice(0, S // 2), slice(S // 2, S))
        xq_plane = sbuf("xq_plane", [P, S], U8)
        nc.vector.tensor_copy(out=xq_plane[:], in_=x_plane[:].indirect(offs_t[:]))
        xq_codes = sbuf("xq_codes", [P, S], U32)
        for points in point_parts:
            nc.vector.tensor_copy(out=xq_codes[:, points], in_=x_codes[:].indirect(entries(offs_t, points)))

        def product(bank, codes, plane, b, points=slice(0, S)):
            features = slice(P * b, P * (b + 1))
            nc.tensor.matmul_mx(
                out=bank[:, points], lhsT=codes[:, features].bitcast(FP8X4), lhsT_scale=plane[:, features],
                rhs=xq_codes[:, points].bitcast(FP8X4), rhs_scale=xq_plane[:, points], start=True, stop=True,
            )

        def per_block(name, shape):
            return [sbuf("%s%d" % (name, b), shape, F32) for b in range(BLOCKS)]

        y = per_block("y", [P, S])
        e = per_block("e", [P, S])
        h = per_block("h", [P, S])
        yc = per_block("yc", [P, V])
        diff = per_block("diff", [P, NEIGHBOURS, V])
        dist = per_block("dist", [P, NEIGHBOURS, V])
        near2 = per_block("near2_", [P, V])
        near3 = per_block("near3_", [P, V])
        excess = per_block("excess", [P, NEIGHBOURS, V])
        weight = per_block("weight", [P, NEIGHBOURS, V])
        term = per_block("term", [P, NEIGHBOURS, V])

        def for_each_neighbour(row):
            return row[:].unsqueeze(1).broadcast_to([P, NEIGHBOURS, V])

        def sum_over_neighbours(bank, summands, b, half):
            for d in range(NEIGHBOURS):
                nc.tensor.matmul(
                    out=bank[:, P * b : P * (b + 1)], lhsT=summands[:, d, P * half : P * (half + 1)],
                    rhs=ident[:], is_transpose=True, start=(d == 0), stop=(d == NEIGHBOURS - 1),
                )

        def queries_and_keys(b):
            y_bank, e_bank = banks[2 * (b % 2) + b // 2], banks[2 * (b % 2) + 1 - b // 2]
            if b == 0:
                for bank, points in zip((num_banks[0], y_bank), point_parts):
                    product(bank, w1_codes, w1_plane, b, points)
                    nc.scalar.activation(out=y[b][:, points], in_=bank[:, points], func=ACT.Copy)
            else:
                product(y_bank, w1_codes, w1_plane, b)
                nc.scalar.activation(out=y[b][:], in_=y_bank[:], func=ACT.Copy)
            product(e_bank, w2_codes, w2_plane, b)
            nc.scalar.copy(out=e[b][:], in_=e_bank[:])
            if b < CENTRES_ON_VECTOR:
                nc.vector.tensor_copy(out=yc[b][:], in_=y[b][:].indirect(cen_t[:]))
            else:
                nc.scalar.activation(out=yc[b][:], in_=y[b][:].indirect(cen_t[:]), func=ACT.Copy)

        def differences(b):
            if b < LAST:
                for d in range(NEIGHBOURS):
                    nc.vector.tensor_tensor(out=diff[b][:, d, :], in0=e[b][:].indirect(pos_t[d][:]), in1=yc[b][:], op=ALU.subtract)
            else:
                keys = sbuf("keys", [P, NEIGHBOURS, V], F32)
                for d in range(NEIGHBOURS):
                    nc.scalar.activation(out=keys[:, d, :], in_=e[b][:].indirect(pos_t[d][:]), func=ACT.Copy)
                nc.vector.tensor_tensor(out=diff[b][:], in0=keys[:], in1=for_each_neighbour(yc[b]), op=ALU.subtract)

        def distances(b):
            nc.scalar.activation(out=dist[b][:], in_=diff[b][:], func=ACT.Abs)

        def shift(b):
            nc.vector.tensor_tensor(out=near2[b][:], in0=dist[b][:, 0, :], in1=dist[b][:, 1, :], op=ALU.min)
            nc.vector.tensor_tensor(out=near3[b][:], in0=near2[b][:], in1=dist[b][:, 2, :], op=ALU.min)
            nc.vector.tensor_tensor(out=excess[b][:], in0=dist[b][:], in1=for_each_neighbour(near3[b]), op=ALU.subtract)

        def weights(b):
            nc.scalar.activation(out=weight[b][:], in_=excess[b][:], func=ACT.Exp, scale=-1.0)
            for half in range(HALVES):
                sum_over_neighbours(den_banks[half], weight[b], b, half)

        def values(b):
            product(banks[b], w3_codes, w3_plane, b)
            nc.scalar.copy(out=h[b][:], in_=banks[b][:])

        def weighted_values(b):
            for d in range(NEIGHBOURS):
                nc.vector.tensor_tensor(out=term[b][:, d, :], in0=h[b][:].indirect(pos_t[d][:]), in1=weight[b][:, d, :], op=ALU.mult)
            for half in range(HALVES):
                sum_over_neighbours(num_banks[half], term[b], b, half)

        for b in range(BLOCKS):
            queries_and_keys(b)
            differences(b)
        distances(0)

        w3_grouped = sbuf("w3_grouped", [P, H * PACK], BF16, reuses="diff0")
        w3_codes = sbuf("w3_codes", [P, H], U32)
        w3_plane = sbuf("w3_plane", [P, H], U8)
        grouped_lines = w3_grouped[:].rearrange("p (c i t) -> p c t i", i=LINE, t=PACK)
        raw_lines = w3_raw[:].rearrange("p t (c i) -> p c t i", i=LINE)
        split = W3_COLUMNS_ON_SCALAR // LINE
        nc.scalar.copy(out=grouped_lines[:, 0:split], in_=raw_lines[:, 0:split])
        nc.vector.tensor_copy(out=grouped_lines[:, split : H // LINE], in_=raw_lines[:, split : H // LINE])
        nc.vector.quantize_mx(out=w3_codes[:].bitcast(FP8X4), scales=w3_plane[:], in_=w3_grouped[:])

        w4_plane_dealt = sbuf("w4_plane_dealt", [P, N], U8)
        nc.vector.tensor_copy(out=w4_plane_dealt[:].rearrange("p (t m) -> p t m", t=PACK), in_=w4_plane.rearrange("p (m t) -> p t m", t=PACK))

        for b in range(1, BLOCKS):
            distances(b)

        for b in range(BLOCKS):
            shift(b)
            values(b)
            weights(b)
        for b in range(LAST):
            weighted_values(b)

        root = [sbuf("root%d" % half, [P, H], F32) for half in range(HALVES)]
        inverse = [sbuf("inverse%d" % half, [P, H], F32) for half in range(HALVES)]
        for half in range(HALVES):
            nc.scalar.activation(out=root[half][:], in_=den_banks[half][:], func=ACT.Abs_reciprocal_sqrt)
            nc.scalar.activation(out=inverse[half][:], in_=root[half][:], func=ACT.Square)

        centre_halves = [slice(P * half, P * (half + 1)) for half in range(HALVES)]
        picked = sbuf("picked", [P, NEIGHBOURS, P], F32, reuses="excess%d" % LAST)
        for d in range(NEIGHBOURS):
            nc.scalar.activation(out=picked[:, d, :], in_=h[LAST][:].indirect(entries(pos_t[d], centre_halves[1])), func=ACT.Copy)

        w4_dealt = sbuf("w4_dealt", [P, N], U32, reuses="root1")
        nc.scalar.copy(out=w4_dealt[:].rearrange("p (t m) -> p m t", t=PACK), in_=w4_codes[:].rearrange("p (m t) -> p m t", t=PACK))

        z_rows = [sbuf("z_rows%d" % half, [P, H], BF16) for half in range(HALVES)]

        def divide(half, numerators, features):
            quads = slice(features.start // PACK, features.stop // PACK)
            nc.vector.tensor_tensor(
                out=z_rows[half][:].rearrange("v (u p j) -> v p u j", u=2, j=2)[:, quads],
                in0=numerators[:].rearrange("v (p u j) -> v p u j", u=2, j=2)[:, quads],
                in1=inverse[half][:].rearrange("v (p u j) -> v p u j", u=2, j=2)[:, quads],
                op=ALU.mult,
            )

        for half, centres in enumerate(centre_halves):
            if half == 0:
                for d in range(NEIGHBOURS):
                    nc.vector.tensor_tensor(
                        out=term[LAST][:, d, centres], in0=h[LAST][:].indirect(entries(pos_t[d], centres)),
                        in1=weight[LAST][:, d, centres], op=ALU.mult,
                    )
            else:
                nc.vector.tensor_tensor(out=term[LAST][:, :, centres], in0=picked[:], in1=weight[LAST][:, :, centres], op=ALU.mult)
            sum_over_neighbours(last_num_banks[half], term[LAST], LAST, half)
            divide(half, num_banks[half], slice(0, P * LAST))

        out_plane = sbuf("out_plane", [P, V], U8)
        out_codes = sbuf("out_codes", [P, V], U32)
        for half, centres in enumerate(centre_halves):
            divide(half, last_num_banks[half], slice(P * LAST, H))

            pairs = z_rows[half][:].bitcast(F32)
            for u in range(2):
                nc.tensor.transpose(turn_banks[half][:, P * u : P * (u + 1)], pairs[:, P * u : P * (u + 1)], ident[:])
            z_grouped = sbuf("z_grouped%d" % half, [P, P * PACK], BF16)
            nc.scalar.copy(
                out=z_grouped[:].bitcast(F32).rearrange("p (v u) -> p v u", u=2),
                in_=turn_banks[half][:, 0 : 2 * P].rearrange("p (u v) -> p v u", u=2),
            )
            z_codes = sbuf("z_codes%d" % half, [P, P], U32)
            z_plane = sbuf("z_plane%d" % half, [P, P], U8)
            nc.vector.quantize_mx(out=z_codes[:].bitcast(FP8X4), scales=z_plane[:], in_=z_grouped[:])

            out_banks = (den_banks[half], num_banks[half])
            for t in range(PACK):
                rows = slice(P * t, P * (t + 1))
                nc.tensor.matmul_mx(
                    out=out_banks[t // 2][:, P * (t % 2) : P * (t % 2 + 1)],
                    lhsT=w4_dealt[:, rows].bitcast(FP8X4), lhsT_scale=w4_plane_dealt[:, rows],
                    rhs=z_codes[:].bitcast(FP8X4), rhs_scale=z_plane[:], start=True, stop=True,
                )
            result = sbuf("result%d" % half, [P, PACK, P], F32)
            for j, bank in enumerate(out_banks):
                nc.scalar.copy(out=result[:, 2 * j : 2 * j + 2, :], in_=bank[:, 0 : 2 * P].rearrange("p (t v) -> p t v", t=2))
            nc.sync.dma_start(out=out_0.rearrange("(p t) v -> p t v", t=PACK)[:, :, centres], in_=result[:])

            out_grouped = sbuf("out_grouped%d" % half, [P, P * PACK], BF16)
            nc.vector.tensor_copy(
                out=out_grouped[:].rearrange("p (c i t) -> p c t i", i=LINE, t=PACK), in_=result[:].rearrange("p t (c i) -> p c t i", i=LINE)
            )
            nc.vector.quantize_mx(out=out_codes[:, centres].bitcast(FP8X4), scales=out_plane[:, centres], in_=out_grouped[:])
            nc.sync.dma_start(out=out_1[0].rearrange("p n t -> p (n t)").bitcast(I32)[:, centres], in_=out_codes[:, centres].bitcast(I32))

        for q in range(QUADRANTS):
            queue = nc.scalar if q % 2 else nc.sync
            queue.dma_start(out=out_2[0][4 * q : 4 * q + 4, :].bitcast(I32), in_=out_plane[32 * q : 32 * q + 4, :].bitcast(I32))
